import numpy as np
import ml_dtypes


def mxq(x, axis, fmt="e4m3"):
    dtype, down = {"e4m3": (ml_dtypes.float8_e4m3fn, 7), "e5m2": (ml_dtypes.float8_e5m2, 14)}[fmt]
    v = np.moveaxis(np.asarray(x, np.float32).astype(ml_dtypes.bfloat16).astype(np.float64), axis, -1)
    blocks = v.reshape(v.shape[:-1] + (-1, 32))
    amax = np.abs(blocks).max(-1, keepdims=True)
    byte = np.maximum(np.where(amax > 0, np.frexp(amax)[1] - 1 + 127, 0) - down, 1)
    scale = np.exp2(byte - 127.0)
    codes = (blocks / scale).astype(np.float32).astype(dtype).astype(np.float64)
    return np.moveaxis((codes * scale).reshape(v.shape), -1, axis)


WIDE = False


def mx_kscale(k):
    if not WIDE:
        return np.ones(k)
    levels = np.array([10, -10, 5, -5, 0])
    if k % 512:
        return np.exp2(np.random.permutation(np.resize(levels, k // 32))).repeat(32)
    a = np.empty((k // 512, 16))
    for p in range(k // 512):
        a[p, :8] = np.random.permutation(np.resize(levels, 8))
        for g in range(8):
            far = levels[np.abs(levels - a[p, g]) >= 10]
            a[p, g + 8] = far[np.random.randint(len(far))]
    return np.exp2(a.ravel()).repeat(32)


def f64(x):
    return np.asarray(x).astype(np.float64)


def striped(idx):
    return np.tile(idx.reshape(-1, 16).T, (8, 1)).astype(np.uint16)


def unstriped(offs):
    return offs[:16].T.reshape(-1).astype(np.int64)


def striped8(idx):
    return np.concatenate([x.reshape(-1, 16).T for x in idx]).astype(np.uint16)


def runs(offs, k):
    lists = np.stack([offs[16 * r : 16 * r + 16].T.reshape(-1) for r in range(8)]).astype(np.int64)
    return lists[np.arange(k) % 512 // 64]


def pack_weight(w):
    k, n = w.shape
    w = f64(np.asarray(w, np.float32).astype(ml_dtypes.bfloat16)).reshape(k // 32, 32, n)
    amax = np.abs(w).max(1)
    byte = np.clip(np.where(amax > 0, np.frexp(amax)[1] - 1 + 127 - 7, 1), 1, 254)
    scaled = (w * np.exp2(127.0 - byte)[:, None, :]).reshape(k, n).astype(np.float32)
    words = np.ascontiguousarray(scaled.reshape(k // 512, 128, 4, n).transpose(0, 1, 3, 2)).astype(ml_dtypes.float8_e4m3fn).view(np.uint8)
    return words, np.ascontiguousarray(byte.astype(np.uint8).reshape(k // 512, 16, n))


def unpack_weight(words, scales):
    g, p, n, _ = words.shape
    vals = np.ascontiguousarray(words).view(ml_dtypes.float8_e4m3fn).astype(np.float64) * np.repeat(np.exp2(scales.astype(np.float64) - 127.0), 8, axis=1)[..., None]
    return vals.transpose(0, 1, 3, 2).reshape(g * 512, n)


def sigmoid(v):
    return 1.0 / (1.0 + np.exp(-np.maximum(v, -700.0)))


K, T, S, N, G, H = 512, 1024, 512, 512, 2048, 512


def setup_inputs():
    n = np.random.standard_normal
    s = mx_kscale(K)[:, None]
    u = mx_kscale(S)
    packed_xT = pack_weight(n((K, T)) * s)
    packed_dT = pack_weight(n((K, G)) / s)
    return {
        "x_words": packed_xT[0],
        "x_scales": packed_xT[1],
        "d_words": packed_dT[0],
        "d_scales": packed_dT[1],
        "gn": (np.random.uniform(0.5, 1.5, (H, 1)) * u[:, None]).astype(np.float32),
        "w1": (n((H, N)) / np.sqrt(H) / u[:, None]).astype(np.float32),
        "offs": striped(np.random.permutation(T)[:S]),
        "k1": striped8(np.random.randint(0, G, (8, H))),
        "two": striped(np.random.permutation(T)[:S]),
        "k2": striped8(np.random.randint(0, G, (8, H))),
        "n1": striped(np.random.permutation(S)),
        "n2": striped(np.random.permutation(S)),
        "n3": striped(np.random.randint(0, S, G)),
    }


def reference(x_words, x_scales, d_words, d_scales, gn, w1, offs, k1, two, k2, n1, n2, n3):
    d_k1 = unpack_weight(d_words, d_scales)[np.arange(K)[:, None], runs(k1, K)]
    xq = unpack_weight(x_words, x_scales)[:, unstriped(offs)]
    a = 0.0625 * (d_k1.T @ xq)
    d_k2 = unpack_weight(d_words, d_scales)[np.arange(K)[:, None], runs(k2, K)]
    x_two = unpack_weight(x_words, x_scales)[:, unstriped(two)]
    b = 0.0625 * (d_k2.T @ x_two)
    z = f64(gn) * (a * (sigmoid(b[:, unstriped(n2)])) - (0.5 * a[:, unstriped(n1)]))
    h = mxq(f64(w1), 0, "e4m3").T @ mxq(z, 0, "e4m3")
    mb = h[:, unstriped(n3)]
    mx = mb.reshape(N, S, 4).max(axis=2)
    mn = mb.reshape(N, S, 4).min(axis=2)
    return np.maximum(np.minimum(1.5 * h, mx), mn)

@@ -1,0 +1,204 @@
+from contextlib import ExitStack
+
+import concourse.mybir as mybir
+
+K, T, S, N, G, H = 512, 1024, 512, 512, 2048, 512
+FLOPS = 2 * K * H * S * 2 + 2 * H * N * S
+
+F32 = mybir.dt.float32
+BF16 = mybir.dt.bfloat16
+I32 = mybir.dt.int32
+U32 = mybir.dt.uint32
+U16 = mybir.dt.uint16
+U8 = mybir.dt.uint8
+FP8X4 = mybir.dt.float8_e4m3fn_x4
+ALU = mybir.AluOpType
+ACT = mybir.ActivationFunctionType
+
+P = 128
+HALF = S // 2
+SPARE = 16
+PIECE = 512
+
+
+def tile_picked_twpqgatebgclip_none_p_kernel(
+    tc, x_words, x_scales, d_words, d_scales, gn, w1, offs, k1, two, k2, n1, n2, n3, out
+):
+    nc = tc.nc
+    with ExitStack() as ctx:
+        keep = ctx.enter_context(tc.tile_pool(name="keep", bufs=1))
+        psum = ctx.enter_context(tc.psum_pool(name="psum", bufs=1))
+
+        def load_list(name, source):
+            tile = keep.tile(list(source.shape), U16, name=name)
+            nc.sync.dma_start(tile[:], source)
+            return tile
+
+        def load_scale_rows(name, source, width):
+            tile = keep.tile([P, width], U8, name=name)
+            rows = source[0].bitcast(I32)
+            nc.sync.dma_start(tile[:].bitcast(I32), rows.unsqueeze(1).to_broadcast([16, 8, width // 4]))
+            return tile
+
+        def load_words(name, source, width):
+            tile = keep.tile([P, width], I32, name=name)
+            nc.sync.dma_start(tile[:], source[0].rearrange("p n t -> p (n t)").bitcast(I32))
+            return tile
+
+        k2_t = load_list("k2_t", k2)
+        d_byte_table = load_scale_rows("d_byte_table", d_scales, G)
+        two_t = load_list("two_t", two)
+        x_byte_table = load_scale_rows("x_byte_table", x_scales, T)
+        k1_t = load_list("k1_t", k1)
+        offs_t = load_list("offs_t", offs)
+        w_raw = keep.tile([P, 4, N], F32, name="w_raw")
+        w_rows = w1.rearrange("(q t r) n -> t q r n", t=4, r=8)
+        for t in range(4):
+            nc.sync.dma_start(w_raw[:, t, :], w_rows[t])
+        d_word_table = load_words("d_word_table", d_words, G)
+        x_word_table = load_words("x_word_table", x_words, T)
+        n2_t = load_list("n2_t", n2)
+        n1_t = load_list("n1_t", n1)
+        n3_t = load_list("n3_t", n3)
+
+        planes = keep.tile([P, 4, S], U8, name="planes", align_bytes=64)
+        nc.gpsimd.memset(planes[:].rearrange("p a s -> p (a s)").bitcast(I32), 0)
+        gn_raw = keep.tile([P, 4, 8], F32, name="gn_raw")
+        gn_rows = gn.rearrange("(q t r) o -> t q r o", t=4, r=8)
+        with nc.allow_non_contiguous_dma(reason="one gain for each partition"):
+            for t in range(4):
+                nc.gpsimd.dma_start(gn_raw[:, t, 0:1], gn_rows[t])
+        gain = keep.tile([P, 4], F32, name="gain")
+        nc.gpsimd.tensor_scalar(gain[:], gn_raw[:, :, 0], 0.0625, 0.0, ALU.mult, ALU.add)
+        h_rows = [keep.tile([P, S + SPARE], F32, name="h_rows%d" % m) for m in range(4)]
+        for m in range(4):
+            nc.gpsimd.memset(h_rows[m][:, S:], 0.0)
+
+        picked_bytes = keep.tile([P, 4, S], U8, name="picked_bytes")
+        for a, (table, entries) in enumerate(
+            [(d_byte_table, k2_t), (x_byte_table, two_t), (d_byte_table, k1_t), (x_byte_table, offs_t)]
+        ):
+            nc.vector.tensor_copy(picked_bytes[:, a, :], table[:].indirect(entries[:]))
+        for r in range(4):
+            nc.scalar.dma_start(
+                planes[r:P:32].rearrange("p a s -> p (a s)").bitcast(I32),
+                picked_bytes[8 * r : P : 32].rearrange("p a s -> p (a s)").bitcast(I32),
+            )
+
+        def coded_product(side, d_list, x_list):
+            d_picked = keep.tile([P, H], I32, name="d_picked%d" % side)
+            nc.vector.tensor_copy(d_picked[:].bitcast(U32), d_word_table[:].bitcast(U32).indirect(d_list[:]))
+            x_picked = keep.tile([P, S], I32, name="x_picked%d" % side, align_bytes=64)
+            nc.vector.tensor_copy(x_picked[:].bitcast(U32), x_word_table[:].bitcast(U32).indirect(x_list[:]))
+            d_dealt = keep.tile([P, H], I32, name="d_dealt%d" % side, align_bytes=64)
+            nc.vector.tensor_copy(
+                d_dealt[:].rearrange("p (t q r) -> p t q r", t=4, r=8),
+                d_picked[:].rearrange("p (q t r) -> p t q r", t=4, r=8),
+            )
+            plane_dealt = keep.tile([P, H], U8, name="plane_dealt%d" % side, align_bytes=64)
+            nc.vector.tensor_copy(
+                plane_dealt[:].bitcast(I32).rearrange("p (t q r) -> p t q r", t=4, r=2),
+                planes[:, 2 * side, :].bitcast(I32).rearrange("p (q t r) -> p t q r", t=4, r=2),
+            )
+            banks = []
+            for t in range(4):
+                bank = psum.tile([P, S], F32, name="bank%d" % (4 * side + t), tag="bank%d" % (4 * side + t))
+                cols = slice(P * t, P * (t + 1))
+                nc.tensor.matmul_mx(
+                    bank[:], d_dealt[:, cols].bitcast(FP8X4), plane_dealt[:, cols],
+                    x_picked[:].bitcast(FP8X4), planes[:, 2 * side + 1, :], start=True, stop=True,
+                )
+                banks.append(bank)
+            return banks
+
+        w_grouped = keep.tile([P, N, 4], BF16, name="w_grouped", align_bytes=64)
+        nc.scalar.copy(
+            w_grouped[:].rearrange("p (c i) t -> p c t i", i=2),
+            w_raw[:].rearrange("p t (c i) -> p c t i", i=2),
+        )
+
+        b_banks = coded_product(0, k2_t, two_t)
+        gate = [keep.tile([P, S], F32, name="gate%d" % t) for t in range(4)]
+        for t in range(4):
+            nc.scalar.activation(gate[t][:], b_banks[t][:], ACT.Sigmoid, scale=0.0625)
+
+        a_banks = coded_product(1, k1_t, offs_t)
+        w_codes = keep.tile([P, N], I32, name="w_codes", align_bytes=64)
+        w_plane = keep.tile([P, N], U8, name="w_plane", align_bytes=64)
+        nc.vector.quantize_mx(w_codes[:].bitcast(FP8X4), w_plane[:], w_grouped[:].rearrange("p n t -> p (n t)"))
+        a_rows = [keep.tile([P, S], F32, name="a_rows%d" % t) for t in range(4)]
+        for t in range(4):
+            nc.scalar.activation(a_rows[t][:], a_banks[t][:], ACT.Copy, scale=gain[:, t : t + 1])
+
+        gated = [keep.tile([P, 4, HALF], F32, name="gated%d" % half) for half in range(2)]
+        other = [keep.tile([P, 4, HALF], F32, name="other%d" % half) for half in range(2)]
+        for half in range(2):
+            cols = slice(HALF * half, HALF * (half + 1))
+            entries = slice(HALF // 16 * half, HALF // 16 * (half + 1))
+            for t in range(4):
+                nc.scalar.activation(other[half][:, t, :], a_rows[t][:].indirect(n1_t[:, entries]), ACT.Copy, scale=-0.5)
+                nc.vector.tensor_tensor(gated[half][:, t, :], gate[t][:].indirect(n2_t[:, entries]), a_rows[t][:, cols], ALU.mult)
+
+        for half in range(2):
+            cols = slice(HALF * half, HALF * (half + 1))
+            z_grouped = keep.tile([P, HALF, 4], BF16, name="z_grouped%d" % half, align_bytes=64)
+            nc.vector.tensor_tensor(
+                z_grouped[:].rearrange("p (c i) t -> p c t i", i=2),
+                gated[half][:].rearrange("p t (c i) -> p c t i", i=2),
+                other[half][:].rearrange("p t (c i) -> p c t i", i=2),
+                ALU.add,
+            )
+            z_codes = keep.tile([P, HALF], I32, name="z_codes%d" % half, align_bytes=64)
+            z_plane = keep.tile([P, HALF], U8, name="z_plane%d" % half, align_bytes=64)
+            nc.vector.quantize_mx(z_codes[:].bitcast(FP8X4), z_plane[:], z_grouped[:].rearrange("p n t -> p (n t)"))
+            for m in range(4):
+                bank = psum.tile([P, HALF], F32, name="h_bank%d" % (4 * half + m), tag="bank%d" % (4 * half + m))
+                rows = slice(P * m, P * (m + 1))
+                nc.tensor.matmul_mx(
+                    bank[:], w_codes[:, rows].bitcast(FP8X4), w_plane[:, rows],
+                    z_codes[:].bitcast(FP8X4), z_plane[:], start=True, stop=True,
+                )
+                if half == 0 or m == 0:
+                    nc.scalar.copy(h_rows[m][:, cols], bank[:])
+                else:
+                    nc.vector.tensor_copy(h_rows[m][:, cols], bank[:])
+
+        units = [(0, 0, 128), (0, 128, 128), (0, 256, 256)]
+        units = units + [(m, j0, 256) for m in (1, 2) for j0 in (0, 256)]
+        units = units + [(3, 0, 256), (3, 256, 128), (3, 384, 64), (3, 448, 64)]
+        results = [keep.tile([P, S], F32, name="result%d" % m) for m in range(4)]
+
+        def finish(unit, capped, smallest):
+            m, j0, width = unit
+            nc.vector.tensor_tensor(results[m][:, j0 : j0 + width], capped[:], smallest[:], ALU.max)
+            if m == 3 or j0 + width == S:
+                lo = j0 if m == 3 else 0
+                nc.sync.dma_start(out[P * m : P * (m + 1), lo : j0 + width], results[m][:, lo : j0 + width])
+
+        pending = None
+        for u, unit in enumerate(units):
+            m, j0, width = unit
+            members = keep.tile([P, width, 4], F32, name="members%d" % u)
+            flat = members[:].rearrange("p j t -> p (j t)")
+            piece = min(PIECE, 4 * width)
+            for e0 in range(0, 4 * width, piece):
+                first = (4 * j0 + e0) // 16
+                looked_up = h_rows[m][:].indirect(n3_t[:, first : first + piece // 16])
+                if u == 1:
+                    nc.vector.tensor_copy(flat[:, e0 : e0 + piece], looked_up)
+                else:
+                    nc.scalar.activation(flat[:, e0 : e0 + piece], looked_up, ACT.Copy)
+            pair_max = keep.tile([P, width, 2], F32, name="pair_max%d" % u)
+            pair_min = keep.tile([P, width, 2], F32, name="pair_min%d" % u)
+            nc.vector.tensor_tensor(pair_max[:], members[:, :, 0:2], members[:, :, 2:4], ALU.max)
+            if pending is not None:
+                finish(*pending)
+            nc.vector.tensor_tensor(pair_min[:], members[:, :, 0:2], members[:, :, 2:4], ALU.min)
+            largest = keep.tile([P, width], F32, name="largest%d" % u)
+            smallest = keep.tile([P, width], F32, name="smallest%d" % u)
+            nc.vector.tensor_tensor(largest[:], pair_max[:, :, 0], pair_max[:, :, 1], ALU.max)
+            nc.vector.tensor_tensor(smallest[:], pair_min[:, :, 0], pair_min[:, :, 1], ALU.min)
+            capped = keep.tile([P, width], F32, name="capped%d" % u)
+            nc.vector.scalar_tensor_tensor(capped[:], h_rows[m][:, j0 : j0 + width], 1.5, largest[:], ALU.mult, ALU.min)
+            pending = (unit, capped, smallest)
+        finish(*pending)

@@ -27,6 +27,7 @@ def tile_picked_twpqgatebgclip_none_p_kernel(
     nc = tc.nc
     with ExitStack() as ctx:
         keep = ctx.enter_context(tc.tile_pool(name="keep", bufs=1))
+        ring = ctx.enter_context(tc.tile_pool(name="ring", bufs=1))
         psum = ctx.enter_context(tc.psum_pool(name="psum", bufs=1))
 
         def load_list(name, source):
@@ -45,85 +46,85 @@ def tile_picked_twpqgatebgclip_none_p_kernel(
             nc.sync.dma_start(tile[:], source[0].rearrange("p n t -> p (n t)").bitcast(I32))
             return tile
 
-        k2_t = load_list("k2_t", k2)
-        d_byte_table = load_scale_rows("d_byte_table", d_scales, G)
         two_t = load_list("two_t", two)
         x_byte_table = load_scale_rows("x_byte_table", x_scales, T)
+        k2_t = load_list("k2_t", k2)
+        d_byte_table = load_scale_rows("d_byte_table", d_scales, G)
         k1_t = load_list("k1_t", k1)
         offs_t = load_list("offs_t", offs)
-        w_raw = keep.tile([P, 4, N], F32, name="w_raw")
-        w_rows = w1.rearrange("(q t r) n -> t q r n", t=4, r=8)
-        for t in range(4):
-            nc.sync.dma_start(w_raw[:, t, :], w_rows[t])
-        d_word_table = load_words("d_word_table", d_words, G)
         x_word_table = load_words("x_word_table", x_words, T)
+        d_word_table = load_words("d_word_table", d_words, G)
         n2_t = load_list("n2_t", n2)
         n1_t = load_list("n1_t", n1)
         n3_t = load_list("n3_t", n3)
 
-        planes = keep.tile([P, 4, S], U8, name="planes", align_bytes=64)
-        nc.gpsimd.memset(planes[:].rearrange("p a s -> p (a s)").bitcast(I32), 0)
+        planes = [keep.tile([P, 2 * S], U8, name="planes%d" % side, align_bytes=64) for side in range(2)]
+        for side in range(2):
+            nc.vector.memset(planes[side][:].bitcast(I32), 0)
         gn_raw = keep.tile([P, 4, 8], F32, name="gn_raw")
         gn_rows = gn.rearrange("(q t r) o -> t q r o", t=4, r=8)
         with nc.allow_non_contiguous_dma(reason="one gain for each partition"):
             for t in range(4):
                 nc.gpsimd.dma_start(gn_raw[:, t, 0:1], gn_rows[t])
-        gain = keep.tile([P, 4], F32, name="gain")
-        nc.gpsimd.tensor_scalar(gain[:], gn_raw[:, :, 0], 0.0625, 0.0, ALU.mult, ALU.add)
         h_rows = [keep.tile([P, S + SPARE], F32, name="h_rows%d" % m) for m in range(4)]
         for m in range(4):
-            nc.gpsimd.memset(h_rows[m][:, S:], 0.0)
+            nc.vector.memset(h_rows[m][:, S:], 0.0)
 
-        picked_bytes = keep.tile([P, 4, S], U8, name="picked_bytes")
-        for a, (table, entries) in enumerate(
-            [(d_byte_table, k2_t), (x_byte_table, two_t), (d_byte_table, k1_t), (x_byte_table, offs_t)]
-        ):
-            nc.vector.tensor_copy(picked_bytes[:, a, :], table[:].indirect(entries[:]))
-        for r in range(4):
-            nc.scalar.dma_start(
-                planes[r:P:32].rearrange("p a s -> p (a s)").bitcast(I32),
-                picked_bytes[8 * r : P : 32].rearrange("p a s -> p (a s)").bitcast(I32),
+        def pick_bytes(side, d_list, x_list):
+            picked = ring.tile([P, 2 * S], U8, name="picked_bytes%d" % side, align_bytes=64, offset=[8192, 3072][side])
+            nc.vector.tensor_copy(picked[:, S:], x_byte_table[:].indirect(x_list[:]))
+            nc.vector.tensor_copy(picked[:, :S], d_byte_table[:].indirect(d_list[:]))
+            dealt = keep.tile([P, 2 * S], U8, name="dealt_bytes%d" % side)
+            nc.vector.tensor_copy(
+                dealt[:, :S].bitcast(I32).rearrange("p (t q r) -> p t q r", t=4, r=2),
+                picked[:, :S].bitcast(I32).rearrange("p (q t r) -> p t q r", t=4, r=2),
             )
+            nc.vector.tensor_copy(dealt[:, S:].bitcast(I32), picked[:, S:].bitcast(I32))
+            for r in range(4):
+                nc.sync.dma_start(planes[side][r:P:32, :].bitcast(I32), dealt[8 * r : P : 32, :].bitcast(I32))
 
         def coded_product(side, d_list, x_list):
-            d_picked = keep.tile([P, H], I32, name="d_picked%d" % side)
+            d_picked = ring.tile([P, H], I32, name="d_picked%d" % side, align_bytes=64, offset=1536)
             nc.vector.tensor_copy(d_picked[:].bitcast(U32), d_word_table[:].bitcast(U32).indirect(d_list[:]))
-            x_picked = keep.tile([P, S], I32, name="x_picked%d" % side, align_bytes=64)
+            x_picked = ring.tile([P, S], I32, name="x_picked%d" % side, align_bytes=64, offset=[6144, 3584][side])
             nc.vector.tensor_copy(x_picked[:].bitcast(U32), x_word_table[:].bitcast(U32).indirect(x_list[:]))
             d_dealt = keep.tile([P, H], I32, name="d_dealt%d" % side, align_bytes=64)
             nc.vector.tensor_copy(
                 d_dealt[:].rearrange("p (t q r) -> p t q r", t=4, r=8),
                 d_picked[:].rearrange("p (q t r) -> p t q r", t=4, r=8),
             )
-            plane_dealt = keep.tile([P, H], U8, name="plane_dealt%d" % side, align_bytes=64)
-            nc.vector.tensor_copy(
-                plane_dealt[:].bitcast(I32).rearrange("p (t q r) -> p t q r", t=4, r=2),
-                planes[:, 2 * side, :].bitcast(I32).rearrange("p (q t r) -> p t q r", t=4, r=2),
-            )
             banks = []
             for t in range(4):
                 bank = psum.tile([P, S], F32, name="bank%d" % (4 * side + t), tag="bank%d" % (4 * side + t))
                 cols = slice(P * t, P * (t + 1))
                 nc.tensor.matmul_mx(
-                    bank[:], d_dealt[:, cols].bitcast(FP8X4), plane_dealt[:, cols],
-                    x_picked[:].bitcast(FP8X4), planes[:, 2 * side + 1, :], start=True, stop=True,
+                    bank[:], d_dealt[:, cols].bitcast(FP8X4), planes[side][:, cols],
+                    x_picked[:].bitcast(FP8X4), planes[side][:, S:], start=True, stop=True,
                 )
                 banks.append(bank)
             return banks
 
-        w_grouped = keep.tile([P, N, 4], BF16, name="w_grouped", align_bytes=64)
-        nc.scalar.copy(
-            w_grouped[:].rearrange("p (c i) t -> p c t i", i=2),
-            w_raw[:].rearrange("p t (c i) -> p c t i", i=2),
-        )
-
+        pick_bytes(0, k2_t, two_t)
+        w_raw = ring.tile([P, 4, N], F32, name="w_raw", align_bytes=64, offset=8192)
+        w_rows = w1.rearrange("(q t r) n -> t q r n", t=4, r=8)
+        for t in range(4):
+            nc.sync.dma_start(w_raw[:, t, :], w_rows[t])
         b_banks = coded_product(0, k2_t, two_t)
         gate = [keep.tile([P, S], F32, name="gate%d" % t) for t in range(4)]
         for t in range(4):
             nc.scalar.activation(gate[t][:], b_banks[t][:], ACT.Sigmoid, scale=0.0625)
 
+        w_grouped = keep.tile([P, N, 4], BF16, name="w_grouped", align_bytes=64)
+        nc.scalar.copy(
+            w_grouped[:].rearrange("p (c i) t -> p c t i", i=4),
+            w_raw[:].rearrange("p t (c i) -> p c t i", i=4),
+        )
+
+        pick_bytes(1, k1_t, offs_t)
+        gain = ring.tile([P, 4], F32, name="gain", align_bytes=64, offset=6144)
+        nc.vector.tensor_scalar(gain[:], gn_raw[:, :, 0], 0.0625, None, ALU.mult)
         a_banks = coded_product(1, k1_t, offs_t)
-        w_codes = keep.tile([P, N], I32, name="w_codes", align_bytes=64)
+        w_codes = ring.tile([P, N], I32, name="w_codes", align_bytes=64, offset=1536)
         w_plane = keep.tile([P, N], U8, name="w_plane", align_bytes=64)
         nc.vector.quantize_mx(w_codes[:].bitcast(FP8X4), w_plane[:], w_grouped[:].rearrange("p n t -> p (n t)"))
         a_rows = [keep.tile([P, S], F32, name="a_rows%d" % t) for t in range(4)]
@@ -132,22 +133,26 @@ def tile_picked_twpqgatebgclip_none_p_kernel(
 
         gated = [keep.tile([P, 4, HALF], F32, name="gated%d" % half) for half in range(2)]
         other = [keep.tile([P, 4, HALF], F32, name="other%d" % half) for half in range(2)]
-        for half in range(2):
-            cols = slice(HALF * half, HALF * (half + 1))
-            entries = slice(HALF // 16 * half, HALF // 16 * (half + 1))
-            for t in range(4):
-                nc.scalar.activation(other[half][:, t, :], a_rows[t][:].indirect(n1_t[:, entries]), ACT.Copy, scale=-0.5)
-                nc.vector.tensor_tensor(gated[half][:, t, :], gate[t][:].indirect(n2_t[:, entries]), a_rows[t][:, cols], ALU.mult)
+        h_banks = {}
 
-        for half in range(2):
-            cols = slice(HALF * half, HALF * (half + 1))
-            z_grouped = keep.tile([P, HALF, 4], BF16, name="z_grouped%d" % half, align_bytes=64)
+        def half_slices(half):
+            return slice(HALF * half, HALF * (half + 1)), slice(HALF // 16 * half, HALF // 16 * (half + 1))
+
+        def gate_rows(half, t):
+            cols, entries = half_slices(half)
+            nc.vector.tensor_tensor(gated[half][:, t, :], gate[t][:].indirect(n2_t[:, entries]), a_rows[t][:, cols], ALU.mult)
+
+        def combine(half):
+            z_grouped = keep.tile([P, HALF, 4], BF16, name="z_grouped%d" % half, tag="z_grouped", align_bytes=64)
             nc.vector.tensor_tensor(
-                z_grouped[:].rearrange("p (c i) t -> p c t i", i=2),
-                gated[half][:].rearrange("p t (c i) -> p c t i", i=2),
-                other[half][:].rearrange("p t (c i) -> p c t i", i=2),
+                z_grouped[:].rearrange("p (c i) t -> p c t i", i=4),
+                gated[half][:].rearrange("p t (c i) -> p c t i", i=4),
+                other[half][:].rearrange("p t (c i) -> p c t i", i=4),
                 ALU.add,
             )
+            return z_grouped
+
+        def dense_product(half, z_grouped):
             z_codes = keep.tile([P, HALF], I32, name="z_codes%d" % half, align_bytes=64)
             z_plane = keep.tile([P, HALF], U8, name="z_plane%d" % half, align_bytes=64)
             nc.vector.quantize_mx(z_codes[:].bitcast(FP8X4), z_plane[:], z_grouped[:].rearrange("p n t -> p (n t)"))
@@ -158,36 +163,48 @@ def tile_picked_twpqgatebgclip_none_p_kernel(
                     bank[:], w_codes[:, rows].bitcast(FP8X4), w_plane[:, rows],
                     z_codes[:].bitcast(FP8X4), z_plane[:], start=True, stop=True,
                 )
-                if half == 0 or m == 0:
-                    nc.scalar.copy(h_rows[m][:, cols], bank[:])
-                else:
-                    nc.vector.tensor_copy(h_rows[m][:, cols], bank[:])
+                h_banks[half, m] = bank
 
-        units = [(0, 0, 128), (0, 128, 128), (0, 256, 256)]
-        units = units + [(m, j0, 256) for m in (1, 2) for j0 in (0, 256)]
-        units = units + [(3, 0, 256), (3, 256, 128), (3, 384, 64), (3, 448, 64)]
+        def empty_bank(half, m):
+            nc.scalar.copy(h_rows[m][:, half_slices(half)[0]], h_banks[half, m][:])
+
+        for half in range(2):
+            for t in range(4):
+                looked_up = a_rows[t][:].indirect(n1_t[:, half_slices(half)[1]])
+                nc.scalar.activation(other[half][:, t, :], looked_up, ACT.Copy, scale=-0.5)
+        for t in range(3):
+            gate_rows(0, t)
+            gate_rows(1, t)
+        gate_rows(0, 3)
+        z_first = combine(0)
+        gate_rows(1, 3)
+        dense_product(0, z_first)
+        for m in range(4):
+            empty_bank(0, m)
+        dense_product(1, combine(1))
+
+        units = [(m, j0, 256) for m in range(3) for j0 in (0, 256)] + [(3, 0, 256), (3, 256, 128), (3, 384, 128)]
         results = [keep.tile([P, S], F32, name="result%d" % m) for m in range(4)]
 
         def finish(unit, capped, smallest):
             m, j0, width = unit
             nc.vector.tensor_tensor(results[m][:, j0 : j0 + width], capped[:], smallest[:], ALU.max)
-            if m == 3 or j0 + width == S:
-                lo = j0 if m == 3 else 0
-                nc.sync.dma_start(out[P * m : P * (m + 1), lo : j0 + width], results[m][:, lo : j0 + width])
+            nc.sync.dma_start(out[P * m : P * (m + 1), j0 : j0 + width], results[m][:, j0 : j0 + width])
 
         pending = None
         for u, unit in enumerate(units):
             m, j0, width = unit
+            if j0 == 0:
+                empty_bank(1, m)
             members = keep.tile([P, width, 4], F32, name="members%d" % u)
             flat = members[:].rearrange("p j t -> p (j t)")
-            piece = min(PIECE, 4 * width)
-            for e0 in range(0, 4 * width, piece):
+            for e0 in range(0, 4 * width, PIECE):
                 first = (4 * j0 + e0) // 16
-                looked_up = h_rows[m][:].indirect(n3_t[:, first : first + piece // 16])
-                if u == 1:
-                    nc.vector.tensor_copy(flat[:, e0 : e0 + piece], looked_up)
+                looked_up = h_rows[m][:].indirect(n3_t[:, first : first + PIECE // 16])
+                if u == 0 and e0 == 0:
+                    nc.vector.tensor_copy(flat[:, e0 : e0 + PIECE], looked_up)
                 else:
-                    nc.scalar.activation(flat[:, e0 : e0 + piece], looked_up, ACT.Copy)
+                    nc.scalar.activation(flat[:, e0 : e0 + PIECE], looked_up, ACT.Copy)
             pair_max = keep.tile([P, width, 2], F32, name="pair_max%d" % u)
             pair_min = keep.tile([P, width, 2], F32, name="pair_min%d" % u)
             nc.vector.tensor_tensor(pair_max[:], members[:, :, 0:2], members[:, :, 2:4], ALU.max)

@@ -17,8 +17,9 @@ ACT = mybir.ActivationFunctionType
 
 P = 128
 HALF = S // 2
-SPARE = 16
-PIECE = 512
+SPARE = 528
+GATE_SPARE = 16
+EARLY = 2
 
 
 def tile_picked_twpqgatebgclip_none_p_kernel(
@@ -61,14 +62,14 @@ def tile_picked_twpqgatebgclip_none_p_kernel(
         planes = [keep.tile([P, 2 * S], U8, name="planes%d" % side, align_bytes=64) for side in range(2)]
         for side in range(2):
             nc.vector.memset(planes[side][:].bitcast(I32), 0)
+        h_rows = [keep.tile([P, S + SPARE], F32, name="h_rows%d" % m) for m in range(4)]
+        for m in range(4):
+            nc.gpsimd.memset(h_rows[m][:, S:], 0.0)
         gn_raw = keep.tile([P, 4, 8], F32, name="gn_raw")
         gn_rows = gn.rearrange("(q t r) o -> t q r o", t=4, r=8)
         with nc.allow_non_contiguous_dma(reason="one gain for each partition"):
             for t in range(4):
                 nc.gpsimd.dma_start(gn_raw[:, t, 0:1], gn_rows[t])
-        h_rows = [keep.tile([P, S + SPARE], F32, name="h_rows%d" % m) for m in range(4)]
-        for m in range(4):
-            nc.vector.memset(h_rows[m][:, S:], 0.0)
 
         def pick_bytes(side, d_list, x_list):
             picked = ring.tile([P, 2 * S], U8, name="picked_bytes%d" % side, align_bytes=64, offset=[8192, 3072][side])
@@ -83,25 +84,30 @@ def tile_picked_twpqgatebgclip_none_p_kernel(
             for r in range(4):
                 nc.sync.dma_start(planes[side][r:P:32, :].bitcast(I32), dealt[8 * r : P : 32, :].bitcast(I32))
 
-        def coded_product(side, d_list, x_list):
+        def coded_product(side, d_list, x_list, first_banks):
+            width = S // len(first_banks)
             d_picked = ring.tile([P, H], I32, name="d_picked%d" % side, align_bytes=64, offset=1536)
             nc.vector.tensor_copy(d_picked[:].bitcast(U32), d_word_table[:].bitcast(U32).indirect(d_list[:]))
-            x_picked = ring.tile([P, S], I32, name="x_picked%d" % side, align_bytes=64, offset=[6144, 3584][side])
-            nc.vector.tensor_copy(x_picked[:].bitcast(U32), x_word_table[:].bitcast(U32).indirect(x_list[:]))
             d_dealt = keep.tile([P, H], I32, name="d_dealt%d" % side, align_bytes=64)
             nc.vector.tensor_copy(
                 d_dealt[:].rearrange("p (t q r) -> p t q r", t=4, r=8),
                 d_picked[:].rearrange("p (q t r) -> p t q r", t=4, r=8),
             )
+            x_picked = ring.tile([P, S], I32, name="x_picked%d" % side, align_bytes=64, offset=[6144, 3584][side])
             banks = []
-            for t in range(4):
-                bank = psum.tile([P, S], F32, name="bank%d" % (4 * side + t), tag="bank%d" % (4 * side + t))
-                cols = slice(P * t, P * (t + 1))
-                nc.tensor.matmul_mx(
-                    bank[:], d_dealt[:, cols].bitcast(FP8X4), planes[side][:, cols],
-                    x_picked[:].bitcast(FP8X4), planes[side][:, S:], start=True, stop=True,
-                )
-                banks.append(bank)
+            for part, first_bank in enumerate(first_banks):
+                places = slice(width * part, width * (part + 1))
+                entries = x_list[:, width // 16 * part : width // 16 * (part + 1)]
+                nc.vector.tensor_copy(x_picked[:, places].bitcast(U32), x_word_table[:].bitcast(U32).indirect(entries))
+                for t in range(4):
+                    bank = psum.tile([P, width], F32, name="coded%d_%d_%d" % (side, part, t), tag="bank%d" % (first_bank + t))
+                    cols = slice(P * t, P * (t + 1))
+                    nc.tensor.matmul_mx(
+                        bank[:], d_dealt[:, cols].bitcast(FP8X4), planes[side][:, cols],
+                        x_picked[:, places].bitcast(FP8X4), planes[side][:, S + width * part : S + width * (part + 1)],
+                        start=True, stop=True,
+                    )
+                    banks.append(bank)
             return banks
 
         pick_bytes(0, k2_t, two_t)
@@ -109,30 +115,38 @@ def tile_picked_twpqgatebgclip_none_p_kernel(
         w_rows = w1.rearrange("(q t r) n -> t q r n", t=4, r=8)
         for t in range(4):
             nc.sync.dma_start(w_raw[:, t, :], w_rows[t])
-        b_banks = coded_product(0, k2_t, two_t)
-        gate = [keep.tile([P, S], F32, name="gate%d" % t) for t in range(4)]
+        b_banks = coded_product(0, k2_t, two_t, [0])
+        gate = [keep.tile([P, S + GATE_SPARE], F32, name="gate%d" % t) for t in range(4)]
         for t in range(4):
-            nc.scalar.activation(gate[t][:], b_banks[t][:], ACT.Sigmoid, scale=0.0625)
+            nc.vector.memset(gate[t][:, S:], 0.0)
+            nc.scalar.activation(gate[t][:, :S], b_banks[t][:], ACT.Sigmoid, scale=0.0625)
 
         w_grouped = keep.tile([P, N, 4], BF16, name="w_grouped", align_bytes=64)
-        nc.scalar.copy(
-            w_grouped[:].rearrange("p (c i) t -> p c t i", i=4),
-            w_raw[:].rearrange("p t (c i) -> p c t i", i=4),
-        )
+        for c0 in range(0, N, P):
+            nc.gpsimd.tensor_scalar(
+                w_grouped[:, c0 : c0 + P, :].rearrange("p (c i) t -> p c t i", i=4),
+                w_raw[:, :, c0 : c0 + P].rearrange("p t (c i) -> p c t i", i=4),
+                1.0, 0.0, ALU.mult, ALU.add,
+            )
+        early_gate = ring.tile([P, EARLY, S], F32, name="early_gate", align_bytes=64, offset=16384)
+        for t in range(EARLY):
+            nc.scalar.activation(early_gate[:, t, :], gate[t][:].indirect(n2_t[:]), ACT.Copy)
 
         pick_bytes(1, k1_t, offs_t)
-        gain = ring.tile([P, 4], F32, name="gain", align_bytes=64, offset=6144)
-        nc.vector.tensor_scalar(gain[:], gn_raw[:, :, 0], 0.0625, None, ALU.mult)
-        a_banks = coded_product(1, k1_t, offs_t)
-        w_codes = ring.tile([P, N], I32, name="w_codes", align_bytes=64, offset=1536)
-        w_plane = keep.tile([P, N], U8, name="w_plane", align_bytes=64)
-        nc.vector.quantize_mx(w_codes[:].bitcast(FP8X4), w_plane[:], w_grouped[:].rearrange("p n t -> p (n t)"))
+        gain = ring.tile([P, 16], F32, name="gain", align_bytes=64, offset=8128)
+        nc.vector.tensor_scalar(gain[:, :4], gn_raw[:, :, 0], 0.0625, None, ALU.mult)
+        a_banks = coded_product(1, k1_t, offs_t, [4, 0])
         a_rows = [keep.tile([P, S], F32, name="a_rows%d" % t) for t in range(4)]
-        for t in range(4):
-            nc.scalar.activation(a_rows[t][:], a_banks[t][:], ACT.Copy, scale=gain[:, t : t + 1])
+        for half in range(2):
+            for t in range(4):
+                nc.scalar.activation(
+                    a_rows[t][:, HALF * half : HALF * (half + 1)], a_banks[4 * half + t][:], ACT.Copy, scale=gain[:, t : t + 1]
+                )
 
         gated = [keep.tile([P, 4, HALF], F32, name="gated%d" % half) for half in range(2)]
-        other = [keep.tile([P, 4, HALF], F32, name="other%d" % half) for half in range(2)]
+        other = [ring.tile([P, 4, HALF], F32, name="other%d" % half, offset=[4064, 8160][half]) for half in range(2)]
+        minus_half = keep.tile([P, HALF], F32, name="minus_half")
+        nc.vector.memset(minus_half[:], -0.5)
         h_banks = {}
 
         def half_slices(half):
@@ -140,7 +154,8 @@ def tile_picked_twpqgatebgclip_none_p_kernel(
 
         def gate_rows(half, t):
             cols, entries = half_slices(half)
-            nc.vector.tensor_tensor(gated[half][:, t, :], gate[t][:].indirect(n2_t[:, entries]), a_rows[t][:, cols], ALU.mult)
+            looked_up = early_gate[:, t, cols] if t < EARLY else gate[t][:].indirect(n2_t[:, entries])
+            nc.vector.tensor_tensor(gated[half][:, t, :], looked_up, a_rows[t][:, cols], ALU.mult)
 
         def combine(half):
             z_grouped = keep.tile([P, HALF, 4], BF16, name="z_grouped%d" % half, tag="z_grouped", align_bytes=64)
@@ -157,7 +172,7 @@ def tile_picked_twpqgatebgclip_none_p_kernel(
             z_plane = keep.tile([P, HALF], U8, name="z_plane%d" % half, align_bytes=64)
             nc.vector.quantize_mx(z_codes[:].bitcast(FP8X4), z_plane[:], z_grouped[:].rearrange("p n t -> p (n t)"))
             for m in range(4):
-                bank = psum.tile([P, HALF], F32, name="h_bank%d" % (4 * half + m), tag="bank%d" % (4 * half + m))
+                bank = psum.tile([P, HALF], F32, name="h_bank%d" % (4 * half + m), tag="bank%d" % (4 * (1 - half) + m))
                 rows = slice(P * m, P * (m + 1))
                 nc.tensor.matmul_mx(
                     bank[:], w_codes[:, rows].bitcast(FP8X4), w_plane[:, rows],
@@ -166,24 +181,29 @@ def tile_picked_twpqgatebgclip_none_p_kernel(
                 h_banks[half, m] = bank
 
         def empty_bank(half, m):
-            nc.scalar.copy(h_rows[m][:, half_slices(half)[0]], h_banks[half, m][:])
+            copy = nc.vector.tensor_copy if (half, m) == (1, 1) else nc.scalar.copy
+            copy(h_rows[m][:, half_slices(half)[0]], h_banks[half, m][:])
 
         for half in range(2):
             for t in range(4):
                 looked_up = a_rows[t][:].indirect(n1_t[:, half_slices(half)[1]])
-                nc.scalar.activation(other[half][:, t, :], looked_up, ACT.Copy, scale=-0.5)
-        for t in range(3):
+                if (half, t) != (1, 3):
+                    nc.scalar.activation(other[half][:, t, :], looked_up, ACT.Copy, scale=-0.5)
+        for t in range(4):
             gate_rows(0, t)
+        for t in range(4):
             gate_rows(1, t)
-        gate_rows(0, 3)
+        w_codes = ring.tile([P, N], I32, name="w_codes", align_bytes=64, offset=16384)
+        w_plane = keep.tile([P, N], U8, name="w_plane", align_bytes=64)
+        nc.vector.quantize_mx(w_codes[:].bitcast(FP8X4), w_plane[:], w_grouped[:].rearrange("p n t -> p (n t)"))
         z_first = combine(0)
-        gate_rows(1, 3)
+        nc.vector.tensor_tensor(other[1][:, 3, :], a_rows[3][:].indirect(n1_t[:, half_slices(1)[1]]), minus_half[:], ALU.mult)
         dense_product(0, z_first)
         for m in range(4):
             empty_bank(0, m)
         dense_product(1, combine(1))
 
-        units = [(m, j0, 256) for m in range(3) for j0 in (0, 256)] + [(3, 0, 256), (3, 256, 128), (3, 384, 128)]
+        units = [(m, j0, 256) for m in range(4) for j0 in (0, 256)]
         results = [keep.tile([P, S], F32, name="result%d" % m) for m in range(4)]
 
         def finish(unit, capped, smallest):
@@ -194,17 +214,19 @@ def tile_picked_twpqgatebgclip_none_p_kernel(
         pending = None
         for u, unit in enumerate(units):
             m, j0, width = unit
-            if j0 == 0:
+            if u == 0:
+                empty_bank(1, 0)
+                empty_bank(1, 1)
+            if j0 == 0 and m > 1:
                 empty_bank(1, m)
             members = keep.tile([P, width, 4], F32, name="members%d" % u)
             flat = members[:].rearrange("p j t -> p (j t)")
-            for e0 in range(0, 4 * width, PIECE):
-                first = (4 * j0 + e0) // 16
-                looked_up = h_rows[m][:].indirect(n3_t[:, first : first + PIECE // 16])
-                if u == 0 and e0 == 0:
-                    nc.vector.tensor_copy(flat[:, e0 : e0 + PIECE], looked_up)
-                else:
-                    nc.scalar.activation(flat[:, e0 : e0 + PIECE], looked_up, ACT.Copy)
+            first = 4 * j0 // 16
+            shared = 512 if u == 0 else 0
+            if shared:
+                nc.vector.tensor_copy(flat[:, :shared], h_rows[m][:].indirect(n3_t[:, first : first + shared // 16]))
+            looked_up = h_rows[m][:].indirect(n3_t[:, first + shared // 16 : first + 4 * width // 16])
+            nc.scalar.activation(flat[:, shared:], looked_up, ACT.Copy)
             pair_max = keep.tile([P, width, 2], F32, name="pair_max%d" % u)
             pair_min = keep.tile([P, width, 2], F32, name="pair_min%d" % u)
             nc.vector.tensor_tensor(pair_max[:], members[:, :, 0:2], members[:, :, 2:4], ALU.max)

@@ -16,10 +16,26 @@ ALU = mybir.AluOpType
 ACT = mybir.ActivationFunctionType
 
 P = 128
+PER_COLUMN = 16
 HALF = S // 2
-SPARE = 528
-GATE_SPARE = 16
+B_SIDE, A_SIDE = 0, 1
+
+STRETCH = 256
+H_SPARE = 4 * STRETCH + PER_COLUMN - S
+GATE_SPARE = PER_COLUMN
+
 EARLY = 2
+VECTOR_N1 = (1, 3)
+VECTOR_BANK = (1, 1)
+VECTOR_MEMBERS = 512
+
+D_PICKED_AT = 1536
+BYTES_AT = {B_SIDE: 8192, A_SIDE: 3072}
+X_PICKED_AT = {B_SIDE: 6144, A_SIDE: 3584}
+W_RAW_AT = 8192
+GAIN_AT = 8128
+OTHER_MEET = GAIN_AT + 32
+EARLY_AT = 16384
 
 
 def tile_picked_twpqgatebgclip_none_p_kernel(
@@ -28,7 +44,7 @@ def tile_picked_twpqgatebgclip_none_p_kernel(
     nc = tc.nc
     with ExitStack() as ctx:
         keep = ctx.enter_context(tc.tile_pool(name="keep", bufs=1))
-        ring = ctx.enter_context(tc.tile_pool(name="ring", bufs=1))
+        shared = ctx.enter_context(tc.tile_pool(name="shared", bufs=1))
         psum = ctx.enter_context(tc.psum_pool(name="psum", bufs=1))
 
         def load_list(name, source):
@@ -47,6 +63,12 @@ def tile_picked_twpqgatebgclip_none_p_kernel(
             nc.sync.dma_start(tile[:], source[0].rearrange("p n t -> p (n t)").bitcast(I32))
             return tile
 
+        def places_of(half):
+            return slice(HALF * half, HALF * (half + 1))
+
+        def entries_of(half):
+            return slice(HALF // PER_COLUMN * half, HALF // PER_COLUMN * (half + 1))
+
         two_t = load_list("two_t", two)
         x_byte_table = load_scale_rows("x_byte_table", x_scales, T)
         k2_t = load_list("k2_t", k2)
@@ -62,7 +84,7 @@ def tile_picked_twpqgatebgclip_none_p_kernel(
         planes = [keep.tile([P, 2 * S], U8, name="planes%d" % side, align_bytes=64) for side in range(2)]
         for side in range(2):
             nc.vector.memset(planes[side][:].bitcast(I32), 0)
-        h_rows = [keep.tile([P, S + SPARE], F32, name="h_rows%d" % m) for m in range(4)]
+        h_rows = [keep.tile([P, S + H_SPARE], F32, name="h_rows%d" % m) for m in range(4)]
         for m in range(4):
             nc.gpsimd.memset(h_rows[m][:, S:], 0.0)
         gn_raw = keep.tile([P, 4, 8], F32, name="gn_raw")
@@ -72,7 +94,7 @@ def tile_picked_twpqgatebgclip_none_p_kernel(
                 nc.gpsimd.dma_start(gn_raw[:, t, 0:1], gn_rows[t])
 
         def pick_bytes(side, d_list, x_list):
-            picked = ring.tile([P, 2 * S], U8, name="picked_bytes%d" % side, align_bytes=64, offset=[8192, 3072][side])
+            picked = shared.tile([P, 2 * S], U8, name="picked_bytes%d" % side, align_bytes=64, offset=BYTES_AT[side])
             nc.vector.tensor_copy(picked[:, S:], x_byte_table[:].indirect(x_list[:]))
             nc.vector.tensor_copy(picked[:, :S], d_byte_table[:].indirect(d_list[:]))
             dealt = keep.tile([P, 2 * S], U8, name="dealt_bytes%d" % side)
@@ -86,85 +108,80 @@ def tile_picked_twpqgatebgclip_none_p_kernel(
 
         def coded_product(side, d_list, x_list, first_banks):
             width = S // len(first_banks)
-            d_picked = ring.tile([P, H], I32, name="d_picked%d" % side, align_bytes=64, offset=1536)
+            d_picked = shared.tile([P, H], I32, name="d_picked%d" % side, align_bytes=64, offset=D_PICKED_AT)
             nc.vector.tensor_copy(d_picked[:].bitcast(U32), d_word_table[:].bitcast(U32).indirect(d_list[:]))
             d_dealt = keep.tile([P, H], I32, name="d_dealt%d" % side, align_bytes=64)
             nc.vector.tensor_copy(
                 d_dealt[:].rearrange("p (t q r) -> p t q r", t=4, r=8),
                 d_picked[:].rearrange("p (q t r) -> p t q r", t=4, r=8),
             )
-            x_picked = ring.tile([P, S], I32, name="x_picked%d" % side, align_bytes=64, offset=[6144, 3584][side])
+            x_picked = shared.tile([P, S], I32, name="x_picked%d" % side, align_bytes=64, offset=X_PICKED_AT[side])
             banks = []
             for part, first_bank in enumerate(first_banks):
                 places = slice(width * part, width * (part + 1))
-                entries = x_list[:, width // 16 * part : width // 16 * (part + 1)]
+                entries = x_list[:, width // PER_COLUMN * part : width // PER_COLUMN * (part + 1)]
                 nc.vector.tensor_copy(x_picked[:, places].bitcast(U32), x_word_table[:].bitcast(U32).indirect(entries))
                 for t in range(4):
                     bank = psum.tile([P, width], F32, name="coded%d_%d_%d" % (side, part, t), tag="bank%d" % (first_bank + t))
-                    cols = slice(P * t, P * (t + 1))
+                    features = slice(P * t, P * (t + 1))
                     nc.tensor.matmul_mx(
-                        bank[:], d_dealt[:, cols].bitcast(FP8X4), planes[side][:, cols],
+                        bank[:], d_dealt[:, features].bitcast(FP8X4), planes[side][:, features],
                         x_picked[:, places].bitcast(FP8X4), planes[side][:, S + width * part : S + width * (part + 1)],
                         start=True, stop=True,
                     )
                     banks.append(bank)
             return banks
 
-        pick_bytes(0, k2_t, two_t)
-        w_raw = ring.tile([P, 4, N], F32, name="w_raw", align_bytes=64, offset=8192)
+        def side_by_side(grouped):
+            return grouped.rearrange("p (c i) t -> p c t i", i=4)
+
+        def tile_by_tile(rows):
+            return rows.rearrange("p t (c i) -> p c t i", i=4)
+
+        pick_bytes(B_SIDE, k2_t, two_t)
+        w_raw = shared.tile([P, 4, N], F32, name="w_raw", align_bytes=64, offset=W_RAW_AT)
         w_rows = w1.rearrange("(q t r) n -> t q r n", t=4, r=8)
         for t in range(4):
             nc.sync.dma_start(w_raw[:, t, :], w_rows[t])
-        b_banks = coded_product(0, k2_t, two_t, [0])
-        gate = [keep.tile([P, S + GATE_SPARE], F32, name="gate%d" % t) for t in range(4)]
+        b_banks = coded_product(B_SIDE, k2_t, two_t, [0])
+        gate = [keep.tile([P, S + GATE_SPARE if t < EARLY else S], F32, name="gate%d" % t) for t in range(4)]
         for t in range(4):
-            nc.vector.memset(gate[t][:, S:], 0.0)
+            if t < EARLY:
+                nc.vector.memset(gate[t][:, S:], 0.0)
             nc.scalar.activation(gate[t][:, :S], b_banks[t][:], ACT.Sigmoid, scale=0.0625)
 
         w_grouped = keep.tile([P, N, 4], BF16, name="w_grouped", align_bytes=64)
         for c0 in range(0, N, P):
             nc.gpsimd.tensor_scalar(
-                w_grouped[:, c0 : c0 + P, :].rearrange("p (c i) t -> p c t i", i=4),
-                w_raw[:, :, c0 : c0 + P].rearrange("p t (c i) -> p c t i", i=4),
+                side_by_side(w_grouped[:, c0 : c0 + P, :]), tile_by_tile(w_raw[:, :, c0 : c0 + P]),
                 1.0, 0.0, ALU.mult, ALU.add,
             )
-        early_gate = ring.tile([P, EARLY, S], F32, name="early_gate", align_bytes=64, offset=16384)
+        early_gate = shared.tile([P, EARLY, S], F32, name="early_gate", align_bytes=64, offset=EARLY_AT)
         for t in range(EARLY):
             nc.scalar.activation(early_gate[:, t, :], gate[t][:].indirect(n2_t[:]), ACT.Copy)
 
-        pick_bytes(1, k1_t, offs_t)
-        gain = ring.tile([P, 16], F32, name="gain", align_bytes=64, offset=8128)
+        pick_bytes(A_SIDE, k1_t, offs_t)
+        gain = shared.tile([P, 16], F32, name="gain", align_bytes=64, offset=GAIN_AT)
         nc.vector.tensor_scalar(gain[:, :4], gn_raw[:, :, 0], 0.0625, None, ALU.mult)
-        a_banks = coded_product(1, k1_t, offs_t, [4, 0])
+        a_banks = coded_product(A_SIDE, k1_t, offs_t, [4, 0])
         a_rows = [keep.tile([P, S], F32, name="a_rows%d" % t) for t in range(4)]
         for half in range(2):
             for t in range(4):
-                nc.scalar.activation(
-                    a_rows[t][:, HALF * half : HALF * (half + 1)], a_banks[4 * half + t][:], ACT.Copy, scale=gain[:, t : t + 1]
-                )
+                nc.scalar.activation(a_rows[t][:, places_of(half)], a_banks[4 * half + t][:], ACT.Copy, scale=gain[:, t : t + 1])
 
         gated = [keep.tile([P, 4, HALF], F32, name="gated%d" % half) for half in range(2)]
-        other = [ring.tile([P, 4, HALF], F32, name="other%d" % half, offset=[4064, 8160][half]) for half in range(2)]
+        other_at = [OTHER_MEET - 4 * HALF * 4, OTHER_MEET]
+        other = [shared.tile([P, 4, HALF], F32, name="other%d" % half, offset=other_at[half]) for half in range(2)]
         minus_half = keep.tile([P, HALF], F32, name="minus_half")
         nc.vector.memset(minus_half[:], -0.5)
         h_banks = {}
 
-        def half_slices(half):
-            return slice(HALF * half, HALF * (half + 1)), slice(HALF // 16 * half, HALF // 16 * (half + 1))
-
-        def gate_rows(half, t):
-            cols, entries = half_slices(half)
-            looked_up = early_gate[:, t, cols] if t < EARLY else gate[t][:].indirect(n2_t[:, entries])
-            nc.vector.tensor_tensor(gated[half][:, t, :], looked_up, a_rows[t][:, cols], ALU.mult)
+        def a_by_n1(half, t):
+            return a_rows[t][:].indirect(n1_t[:, entries_of(half)])
 
         def combine(half):
             z_grouped = keep.tile([P, HALF, 4], BF16, name="z_grouped%d" % half, tag="z_grouped", align_bytes=64)
-            nc.vector.tensor_tensor(
-                z_grouped[:].rearrange("p (c i) t -> p c t i", i=4),
-                gated[half][:].rearrange("p t (c i) -> p c t i", i=4),
-                other[half][:].rearrange("p t (c i) -> p c t i", i=4),
-                ALU.add,
-            )
+            nc.vector.tensor_tensor(side_by_side(z_grouped[:]), tile_by_tile(gated[half][:]), tile_by_tile(other[half][:]), ALU.add)
             return z_grouped
 
         def dense_product(half, z_grouped):
@@ -173,71 +190,67 @@ def tile_picked_twpqgatebgclip_none_p_kernel(
             nc.vector.quantize_mx(z_codes[:].bitcast(FP8X4), z_plane[:], z_grouped[:].rearrange("p n t -> p (n t)"))
             for m in range(4):
                 bank = psum.tile([P, HALF], F32, name="h_bank%d" % (4 * half + m), tag="bank%d" % (4 * (1 - half) + m))
-                rows = slice(P * m, P * (m + 1))
+                block = slice(P * m, P * (m + 1))
                 nc.tensor.matmul_mx(
-                    bank[:], w_codes[:, rows].bitcast(FP8X4), w_plane[:, rows],
+                    bank[:], w_codes[:, block].bitcast(FP8X4), w_plane[:, block],
                     z_codes[:].bitcast(FP8X4), z_plane[:], start=True, stop=True,
                 )
                 h_banks[half, m] = bank
 
         def empty_bank(half, m):
-            copy = nc.vector.tensor_copy if (half, m) == (1, 1) else nc.scalar.copy
-            copy(h_rows[m][:, half_slices(half)[0]], h_banks[half, m][:])
+            copy = nc.vector.tensor_copy if (half, m) == VECTOR_BANK else nc.scalar.copy
+            copy(h_rows[m][:, places_of(half)], h_banks[half, m][:])
 
         for half in range(2):
             for t in range(4):
-                looked_up = a_rows[t][:].indirect(n1_t[:, half_slices(half)[1]])
-                if (half, t) != (1, 3):
-                    nc.scalar.activation(other[half][:, t, :], looked_up, ACT.Copy, scale=-0.5)
-        for t in range(4):
-            gate_rows(0, t)
-        for t in range(4):
-            gate_rows(1, t)
-        w_codes = ring.tile([P, N], I32, name="w_codes", align_bytes=64, offset=16384)
+                if (half, t) != VECTOR_N1:
+                    nc.scalar.activation(other[half][:, t, :], a_by_n1(half, t), ACT.Copy, scale=-0.5)
+        for half in range(2):
+            for t in range(4):
+                gate_by_n2 = early_gate[:, t, places_of(half)] if t < EARLY else gate[t][:].indirect(n2_t[:, entries_of(half)])
+                nc.vector.tensor_tensor(gated[half][:, t, :], gate_by_n2, a_rows[t][:, places_of(half)], ALU.mult)
+        w_codes = shared.tile([P, N], I32, name="w_codes", align_bytes=64, offset=EARLY_AT)
         w_plane = keep.tile([P, N], U8, name="w_plane", align_bytes=64)
         nc.vector.quantize_mx(w_codes[:].bitcast(FP8X4), w_plane[:], w_grouped[:].rearrange("p n t -> p (n t)"))
         z_first = combine(0)
-        nc.vector.tensor_tensor(other[1][:, 3, :], a_rows[3][:].indirect(n1_t[:, half_slices(1)[1]]), minus_half[:], ALU.mult)
+        nc.vector.tensor_tensor(other[VECTOR_N1[0]][:, VECTOR_N1[1], :], a_by_n1(*VECTOR_N1), minus_half[:], ALU.mult)
         dense_product(0, z_first)
         for m in range(4):
             empty_bank(0, m)
         dense_product(1, combine(1))
 
-        units = [(m, j0, 256) for m in range(4) for j0 in (0, 256)]
         results = [keep.tile([P, S], F32, name="result%d" % m) for m in range(4)]
 
-        def finish(unit, capped, smallest):
-            m, j0, width = unit
-            nc.vector.tensor_tensor(results[m][:, j0 : j0 + width], capped[:], smallest[:], ALU.max)
-            nc.sync.dma_start(out[P * m : P * (m + 1), j0 : j0 + width], results[m][:, j0 : j0 + width])
+        def finish(m, j0, capped, smallest):
+            places = slice(j0, j0 + STRETCH)
+            nc.vector.tensor_tensor(results[m][:, places], capped[:], smallest[:], ALU.max)
+            nc.sync.dma_start(out[P * m : P * (m + 1), places], results[m][:, places])
 
         pending = None
-        for u, unit in enumerate(units):
-            m, j0, width = unit
-            if u == 0:
-                empty_bank(1, 0)
-                empty_bank(1, 1)
-            if j0 == 0 and m > 1:
+        for u, (m, j0) in enumerate([(m, j0) for m in range(4) for j0 in range(0, S, STRETCH)]):
+            if j0 == 0 and (1, m) != VECTOR_BANK:
                 empty_bank(1, m)
-            members = keep.tile([P, width, 4], F32, name="members%d" % u)
+            if u == 0:
+                empty_bank(*VECTOR_BANK)
+            members = keep.tile([P, STRETCH, 4], F32, name="members%d" % u)
             flat = members[:].rearrange("p j t -> p (j t)")
-            first = 4 * j0 // 16
-            shared = 512 if u == 0 else 0
-            if shared:
-                nc.vector.tensor_copy(flat[:, :shared], h_rows[m][:].indirect(n3_t[:, first : first + shared // 16]))
-            looked_up = h_rows[m][:].indirect(n3_t[:, first + shared // 16 : first + 4 * width // 16])
-            nc.scalar.activation(flat[:, shared:], looked_up, ACT.Copy)
-            pair_max = keep.tile([P, width, 2], F32, name="pair_max%d" % u)
-            pair_min = keep.tile([P, width, 2], F32, name="pair_min%d" % u)
+            first = 4 * j0 // PER_COLUMN
+            split = VECTOR_MEMBERS if u == 0 else 0
+            if split:
+                nc.vector.tensor_copy(flat[:, :split], h_rows[m][:].indirect(n3_t[:, first : first + split // PER_COLUMN]))
+            rest = n3_t[:, first + split // PER_COLUMN : first + 4 * STRETCH // PER_COLUMN]
+            nc.scalar.activation(flat[:, split:], h_rows[m][:].indirect(rest), ACT.Copy)
+            pair_max = keep.tile([P, STRETCH, 2], F32, name="pair_max%d" % u)
+            pair_min = keep.tile([P, STRETCH, 2], F32, name="pair_min%d" % u)
             nc.vector.tensor_tensor(pair_max[:], members[:, :, 0:2], members[:, :, 2:4], ALU.max)
             if pending is not None:
                 finish(*pending)
             nc.vector.tensor_tensor(pair_min[:], members[:, :, 0:2], members[:, :, 2:4], ALU.min)
-            largest = keep.tile([P, width], F32, name="largest%d" % u)
-            smallest = keep.tile([P, width], F32, name="smallest%d" % u)
+            largest = keep.tile([P, STRETCH], F32, name="largest%d" % u)
+            smallest = keep.tile([P, STRETCH], F32, name="smallest%d" % u)
             nc.vector.tensor_tensor(largest[:], pair_max[:, :, 0], pair_max[:, :, 1], ALU.max)
             nc.vector.tensor_tensor(smallest[:], pair_min[:, :, 0], pair_min[:, :, 1], ALU.min)
-            capped = keep.tile([P, width], F32, name="capped%d" % u)
-            nc.vector.scalar_tensor_tensor(capped[:], h_rows[m][:, j0 : j0 + width], 1.5, largest[:], ALU.mult, ALU.min)
-            pending = (unit, capped, smallest)
+            capped = keep.tile([P, STRETCH], F32, name="capped%d" % u)
+            nc.vector.scalar_tensor_tensor(capped[:], h_rows[m][:, j0 : j0 + STRETCH], 1.5, largest[:], ALU.mult, ALU.min)
+            pending = (m, j0, capped, smallest)
         finish(*pending)

from contextlib import ExitStack

import concourse.mybir as mybir

K, T, S, N, G, H = 512, 1024, 512, 512, 2048, 512
FLOPS = 2 * K * H * S * 2 + 2 * H * N * S

F32 = mybir.dt.float32
BF16 = mybir.dt.bfloat16
I32 = mybir.dt.int32
U32 = mybir.dt.uint32
U16 = mybir.dt.uint16
U8 = mybir.dt.uint8
FP8X4 = mybir.dt.float8_e4m3fn_x4
ALU = mybir.AluOpType
ACT = mybir.ActivationFunctionType

P = 128
PER_COLUMN = 16
HALF = S // 2
B_SIDE, A_SIDE = 0, 1

STRETCH = 256
H_SPARE = 4 * STRETCH + PER_COLUMN - S
GATE_SPARE = PER_COLUMN

EARLY = 2
VECTOR_N1 = (1, 3)
VECTOR_BANK = (1, 1)
VECTOR_MEMBERS = 512

D_PICKED_AT = 1536
BYTES_AT = {B_SIDE: 8192, A_SIDE: 3072}
X_PICKED_AT = {B_SIDE: 6144, A_SIDE: 3584}
W_RAW_AT = 8192
GAIN_AT = 8128
OTHER_MEET = GAIN_AT + 32
EARLY_AT = 16384


def tile_picked_twpqgatebgclip_none_p_kernel(
    tc, x_words, x_scales, d_words, d_scales, gn, w1, offs, k1, two, k2, n1, n2, n3, out
):
    nc = tc.nc
    with ExitStack() as ctx:
        keep = ctx.enter_context(tc.tile_pool(name="keep", bufs=1))
        shared = ctx.enter_context(tc.tile_pool(name="shared", bufs=1))
        psum = ctx.enter_context(tc.psum_pool(name="psum", bufs=1))

        def load_list(name, source):
            tile = keep.tile(list(source.shape), U16, name=name)
            nc.sync.dma_start(tile[:], source)
            return tile

        def load_scale_rows(name, source, width):
            tile = keep.tile([P, width], U8, name=name)
            rows = source[0].bitcast(I32)
            nc.sync.dma_start(tile[:].bitcast(I32), rows.unsqueeze(1).to_broadcast([16, 8, width // 4]))
            return tile

        def load_words(name, source, width):
            tile = keep.tile([P, width], I32, name=name)
            nc.sync.dma_start(tile[:], source[0].rearrange("p n t -> p (n t)").bitcast(I32))
            return tile

        def places_of(half):
            return slice(HALF * half, HALF * (half + 1))

        def entries_of(half):
            return slice(HALF // PER_COLUMN * half, HALF // PER_COLUMN * (half + 1))

        two_t = load_list("two_t", two)
        x_byte_table = load_scale_rows("x_byte_table", x_scales, T)
        k2_t = load_list("k2_t", k2)
        d_byte_table = load_scale_rows("d_byte_table", d_scales, G)
        k1_t = load_list("k1_t", k1)
        offs_t = load_list("offs_t", offs)
        x_word_table = load_words("x_word_table", x_words, T)
        d_word_table = load_words("d_word_table", d_words, G)
        n2_t = load_list("n2_t", n2)
        n1_t = load_list("n1_t", n1)
        n3_t = load_list("n3_t", n3)

        planes = [keep.tile([P, 2 * S], U8, name="planes%d" % side, align_bytes=64) for side in range(2)]
        for side in range(2):
            nc.vector.memset(planes[side][:].bitcast(I32), 0)
        h_rows = [keep.tile([P, S + H_SPARE], F32, name="h_rows%d" % m) for m in range(4)]
        for m in range(4):
            nc.gpsimd.memset(h_rows[m][:, S:], 0.0)
        gn_raw = keep.tile([P, 4, 8], F32, name="gn_raw")
        gn_rows = gn.rearrange("(q t r) o -> t q r o", t=4, r=8)
        with nc.allow_non_contiguous_dma(reason="one gain for each partition"):
            for t in range(4):
                nc.gpsimd.dma_start(gn_raw[:, t, 0:1], gn_rows[t])

        def pick_bytes(side, d_list, x_list):
            picked = shared.tile([P, 2 * S], U8, name="picked_bytes%d" % side, align_bytes=64, offset=BYTES_AT[side])
            nc.vector.tensor_copy(picked[:, S:], x_byte_table[:].indirect(x_list[:]))
            nc.vector.tensor_copy(picked[:, :S], d_byte_table[:].indirect(d_list[:]))
            dealt = keep.tile([P, 2 * S], U8, name="dealt_bytes%d" % side)
            nc.vector.tensor_copy(
                dealt[:, :S].bitcast(I32).rearrange("p (t q r) -> p t q r", t=4, r=2),
                picked[:, :S].bitcast(I32).rearrange("p (q t r) -> p t q r", t=4, r=2),
            )
            nc.vector.tensor_copy(dealt[:, S:].bitcast(I32), picked[:, S:].bitcast(I32))
            for r in range(4):
                nc.sync.dma_start(planes[side][r:P:32, :].bitcast(I32), dealt[8 * r : P : 32, :].bitcast(I32))

        def coded_product(side, d_list, x_list, first_banks):
            width = S // len(first_banks)
            d_picked = shared.tile([P, H], I32, name="d_picked%d" % side, align_bytes=64, offset=D_PICKED_AT)
            nc.vector.tensor_copy(d_picked[:].bitcast(U32), d_word_table[:].bitcast(U32).indirect(d_list[:]))
            d_dealt = keep.tile([P, H], I32, name="d_dealt%d" % side, align_bytes=64)
            nc.vector.tensor_copy(
                d_dealt[:].rearrange("p (t q r) -> p t q r", t=4, r=8),
                d_picked[:].rearrange("p (q t r) -> p t q r", t=4, r=8),
            )
            x_picked = shared.tile([P, S], I32, name="x_picked%d" % side, align_bytes=64, offset=X_PICKED_AT[side])
            banks = []
            for part, first_bank in enumerate(first_banks):
                places = slice(width * part, width * (part + 1))
                entries = x_list[:, width // PER_COLUMN * part : width // PER_COLUMN * (part + 1)]
                nc.vector.tensor_copy(x_picked[:, places].bitcast(U32), x_word_table[:].bitcast(U32).indirect(entries))
                for t in range(4):
                    bank = psum.tile([P, width], F32, name="coded%d_%d_%d" % (side, part, t), tag="bank%d" % (first_bank + t))
                    features = slice(P * t, P * (t + 1))
                    nc.tensor.matmul_mx(
                        bank[:], d_dealt[:, features].bitcast(FP8X4), planes[side][:, features],
                        x_picked[:, places].bitcast(FP8X4), planes[side][:, S + width * part : S + width * (part + 1)],
                        start=True, stop=True,
                    )
                    banks.append(bank)
            return banks

        def side_by_side(grouped):
            return grouped.rearrange("p (c i) t -> p c t i", i=4)

        def tile_by_tile(rows):
            return rows.rearrange("p t (c i) -> p c t i", i=4)

        pick_bytes(B_SIDE, k2_t, two_t)
        w_raw = shared.tile([P, 4, N], F32, name="w_raw", align_bytes=64, offset=W_RAW_AT)
        w_rows = w1.rearrange("(q t r) n -> t q r n", t=4, r=8)
        for t in range(4):
            nc.sync.dma_start(w_raw[:, t, :], w_rows[t])
        b_banks = coded_product(B_SIDE, k2_t, two_t, [0])
        gate = [keep.tile([P, S + GATE_SPARE if t < EARLY else S], F32, name="gate%d" % t) for t in range(4)]
        for t in range(4):
            if t < EARLY:
                nc.vector.memset(gate[t][:, S:], 0.0)
            nc.scalar.activation(gate[t][:, :S], b_banks[t][:], ACT.Sigmoid, scale=0.0625)

        w_grouped = keep.tile([P, N, 4], BF16, name="w_grouped", align_bytes=64)
        for c0 in range(0, N, P):
            nc.gpsimd.tensor_scalar(
                side_by_side(w_grouped[:, c0 : c0 + P, :]), tile_by_tile(w_raw[:, :, c0 : c0 + P]),
                1.0, 0.0, ALU.mult, ALU.add,
            )
        early_gate = shared.tile([P, EARLY, S], F32, name="early_gate", align_bytes=64, offset=EARLY_AT)
        for t in range(EARLY):
            nc.scalar.activation(early_gate[:, t, :], gate[t][:].indirect(n2_t[:]), ACT.Copy)

        pick_bytes(A_SIDE, k1_t, offs_t)
        gain = shared.tile([P, 16], F32, name="gain", align_bytes=64, offset=GAIN_AT)
        nc.vector.tensor_scalar(gain[:, :4], gn_raw[:, :, 0], 0.0625, None, ALU.mult)
        a_banks = coded_product(A_SIDE, k1_t, offs_t, [4, 0])
        a_rows = [keep.tile([P, S], F32, name="a_rows%d" % t) for t in range(4)]
        for half in range(2):
            for t in range(4):
                nc.scalar.activation(a_rows[t][:, places_of(half)], a_banks[4 * half + t][:], ACT.Copy, scale=gain[:, t : t + 1])

        gated = [keep.tile([P, 4, HALF], F32, name="gated%d" % half) for half in range(2)]
        other_at = [OTHER_MEET - 4 * HALF * 4, OTHER_MEET]
        other = [shared.tile([P, 4, HALF], F32, name="other%d" % half, offset=other_at[half]) for half in range(2)]
        minus_half = keep.tile([P, HALF], F32, name="minus_half")
        nc.vector.memset(minus_half[:], -0.5)
        h_banks = {}

        def a_by_n1(half, t):
            return a_rows[t][:].indirect(n1_t[:, entries_of(half)])

        def combine(half):
            z_grouped = keep.tile([P, HALF, 4], BF16, name="z_grouped%d" % half, tag="z_grouped", align_bytes=64)
            nc.vector.tensor_tensor(side_by_side(z_grouped[:]), tile_by_tile(gated[half][:]), tile_by_tile(other[half][:]), ALU.add)
            return z_grouped

        def dense_product(half, z_grouped):
            z_codes = keep.tile([P, HALF], I32, name="z_codes%d" % half, align_bytes=64)
            z_plane = keep.tile([P, HALF], U8, name="z_plane%d" % half, align_bytes=64)
            nc.vector.quantize_mx(z_codes[:].bitcast(FP8X4), z_plane[:], z_grouped[:].rearrange("p n t -> p (n t)"))
            for m in range(4):
                bank = psum.tile([P, HALF], F32, name="h_bank%d" % (4 * half + m), tag="bank%d" % (4 * (1 - half) + m))
                block = slice(P * m, P * (m + 1))
                nc.tensor.matmul_mx(
                    bank[:], w_codes[:, block].bitcast(FP8X4), w_plane[:, block],
                    z_codes[:].bitcast(FP8X4), z_plane[:], start=True, stop=True,
                )
                h_banks[half, m] = bank

        def empty_bank(half, m):
            copy = nc.vector.tensor_copy if (half, m) == VECTOR_BANK else nc.scalar.copy
            copy(h_rows[m][:, places_of(half)], h_banks[half, m][:])

        for half in range(2):
            for t in range(4):
                if (half, t) != VECTOR_N1:
                    nc.scalar.activation(other[half][:, t, :], a_by_n1(half, t), ACT.Copy, scale=-0.5)
        for half in range(2):
            for t in range(4):
                gate_by_n2 = early_gate[:, t, places_of(half)] if t < EARLY else gate[t][:].indirect(n2_t[:, entries_of(half)])
                nc.vector.tensor_tensor(gated[half][:, t, :], gate_by_n2, a_rows[t][:, places_of(half)], ALU.mult)
        w_codes = shared.tile([P, N], I32, name="w_codes", align_bytes=64, offset=EARLY_AT)
        w_plane = keep.tile([P, N], U8, name="w_plane", align_bytes=64)
        nc.vector.quantize_mx(w_codes[:].bitcast(FP8X4), w_plane[:], w_grouped[:].rearrange("p n t -> p (n t)"))
        z_first = combine(0)
        nc.vector.tensor_tensor(other[VECTOR_N1[0]][:, VECTOR_N1[1], :], a_by_n1(*VECTOR_N1), minus_half[:], ALU.mult)
        dense_product(0, z_first)
        for m in range(4):
            empty_bank(0, m)
        dense_product(1, combine(1))

        results = [keep.tile([P, S], F32, name="result%d" % m) for m in range(4)]

        def finish(m, j0, capped, smallest):
            places = slice(j0, j0 + STRETCH)
            nc.vector.tensor_tensor(results[m][:, places], capped[:], smallest[:], ALU.max)
            nc.sync.dma_start(out[P * m : P * (m + 1), places], results[m][:, places])

        pending = None
        for u, (m, j0) in enumerate([(m, j0) for m in range(4) for j0 in range(0, S, STRETCH)]):
            if j0 == 0 and (1, m) != VECTOR_BANK:
                empty_bank(1, m)
            if u == 0:
                empty_bank(*VECTOR_BANK)
            members = keep.tile([P, STRETCH, 4], F32, name="members%d" % u)
            flat = members[:].rearrange("p j t -> p (j t)")
            first = 4 * j0 // PER_COLUMN
            split = VECTOR_MEMBERS if u == 0 else 0
            if split:
                nc.vector.tensor_copy(flat[:, :split], h_rows[m][:].indirect(n3_t[:, first : first + split // PER_COLUMN]))
            rest = n3_t[:, first + split // PER_COLUMN : first + 4 * STRETCH // PER_COLUMN]
            nc.scalar.activation(flat[:, split:], h_rows[m][:].indirect(rest), ACT.Copy)
            pair_max = keep.tile([P, STRETCH, 2], F32, name="pair_max%d" % u)
            pair_min = keep.tile([P, STRETCH, 2], F32, name="pair_min%d" % u)
            nc.vector.tensor_tensor(pair_max[:], members[:, :, 0:2], members[:, :, 2:4], ALU.max)
            if pending is not None:
                finish(*pending)
            nc.vector.tensor_tensor(pair_min[:], members[:, :, 0:2], members[:, :, 2:4], ALU.min)
            largest = keep.tile([P, STRETCH], F32, name="largest%d" % u)
            smallest = keep.tile([P, STRETCH], F32, name="smallest%d" % u)
            nc.vector.tensor_tensor(largest[:], pair_max[:, :, 0], pair_max[:, :, 1], ALU.max)
            nc.vector.tensor_tensor(smallest[:], pair_min[:, :, 0], pair_min[:, :, 1], ALU.min)
            capped = keep.tile([P, STRETCH], F32, name="capped%d" % u)
            nc.vector.scalar_tensor_tensor(capped[:], h_rows[m][:, j0 : j0 + STRETCH], 1.5, largest[:], ALU.mult, ALU.min)
            pending = (m, j0, capped, smallest)
        finish(*pending)
